import numpy as np, ml_dtypes
CORES = [1,9,17,25,129,137,145,153,257,265,273,281,385,393,401,409]
N = 16
T = 16
ROUTE = [[[2,6],[4,9],[7,15],[0,1],[3,10],[10,1],[15,11],[0,4],[0,15],[6,9],[6,14],[2,10],[3,1],[3,5],[14,0],[13,1]],[[1,11],[7,5],[14,9],[15,5],[9,2],[1,9],[7,9],[10,2],[7,12],[9,13],[2,15],[0,5],[14,5],[2,1],[4,8],[1,9]],[[4,12],[1,6],[1,15],[0,10],[11,15],[15,7],[10,7],[7,12],[12,11],[6,4],[11,4],[7,0],[15,0],[3,0],[5,10],[13,7]],[[14,12],[2,10],[13,5],[11,9],[2,6],[4,8],[15,11],[12,2],[1,5],[0,1],[6,10],[12,7],[3,12],[10,6],[4,7],[14,1]],[[14,0],[0,14],[8,0],[2,4],[11,2],[3,7],[10,2],[9,5],[7,2],[3,5],[0,7],[10,11],[11,5],[0,11],[0,5],[3,2]],[[7,12],[15,1],[4,14],[8,6],[6,9],[2,12],[7,1],[10,14],[8,4],[6,15],[9,3],[0,11],[14,4],[8,9],[9,7],[0,14]],[[4,1],[7,13],[7,2],[0,2],[9,4],[9,12],[15,11],[15,0],[15,12],[8,4],[11,3],[11,12],[6,3],[0,11],[0,8],[8,2]],[[7,14],[9,13],[0,3],[12,11],[1,2],[0,11],[13,6],[5,3],[2,5],[12,2],[5,4],[13,14],[12,5],[5,9],[4,14],[0,3]],[[5,8],[10,3],[4,11],[15,4],[13,2],[11,13],[3,7],[4,14],[7,14],[3,6],[9,14],[6,10],[7,8],[1,7],[13,10],[2,14]],[[2,14],[6,2],[0,8],[11,13],[3,13],[6,2],[15,1],[12,14],[13,1],[6,9],[5,10],[14,4],[15,14],[8,11],[2,9],[1,8]],[[1,15],[4,2],[12,6],[6,1],[9,1],[14,11],[2,0],[2,1],[6,15],[2,8],[2,5],[12,6],[7,14],[11,6],[0,14],[9,0]],[[13,9],[10,6],[6,14],[13,14],[6,9],[1,2],[4,5],[1,5],[6,4],[9,0],[2,7],[5,2],[4,3],[14,9],[0,11],[14,4]],[[12,7],[0,10],[14,13],[13,9],[15,7],[10,0],[14,0],[13,7],[13,6],[1,9],[12,0],[14,3],[3,10],[9,14],[12,0],[2,0]],[[15,12],[15,5],[3,14],[7,8],[8,5],[1,6],[14,0],[6,9],[9,8],[4,7],[5,6],[13,6],[1,12],[6,1],[11,9],[12,15]],[[9,8],[14,9],[15,0],[4,3],[13,7],[10,12],[2,10],[1,14],[8,11],[10,15],[4,12],[6,11],[7,8],[4,1],[15,14],[3,4]],[[14,8],[7,14],[7,10],[7,2],[8,11],[1,10],[13,7],[3,6],[13,6],[5,9],[1,4],[5,1],[13,15],[13,1],[13,10],[15,8]]]
ZW = 41
def setup_inputs(rng):
    return {"z": rng.standard_normal((N, 128, ZW), dtype=np.float32).astype(ml_dtypes.bfloat16)}
def reference(z):
    y = np.zeros((N, 128, T), np.float64)
    fill = [0] * N
    for r in range(N):
        for t in range(T):
            for e in ROUTE[r][t]:
                y[r][:, t] += z[e][:, fill[e]].astype(np.float64)
                fill[e] += 1
    return {"y": y.astype(z.dtype)}

@@ -1,0 +1,207 @@
+from concourse.bass import DstId, RemoteDMATransfer
+from concourse.mybir import AluOpType
+
+TOK = 16
+ZCOLS = 41
+WMAX = 8
+
+SCRATCH = {
+    "Z": ("sbuf", [128, ZCOLS], "bfloat16"),
+    "win": ("sbuf", [128, WMAX], "bfloat16"),
+    "AB": ("sbuf", [128, 2 * TOK], "bfloat16"),
+}
+SEMAPHORES = ["ld", "sent", "got", "arr"]
+
+PLAN = {}
+
+
+def split(n, cap=8):
+    size = [1] * n
+    while n:
+        i = min(range(n), key=lambda q: size[q])
+        if sum(size) + size[i] > cap:
+            break
+        size[i] *= 2
+    return size
+
+
+def rows(n):
+    return 128 // min(split(n)) if n else 0
+
+
+def masks(n, base):
+    out, bit = [], base
+    for s in split(n):
+        out.append((((1 << s) - 1) << bit, s))
+        bit += s
+    return out
+
+
+def group_columns(kind, host_of, h, width, max_direct):
+    n = len(kind)
+    memo = {}
+
+    def sorts(ns, nself, diag, odd, hm):
+        out = []
+        if not diag and ns <= 4 and nself <= 4:
+            if not odd:
+                out.append("ONS")
+            out.append("ONM")
+        if ns + nself <= 4:
+            for hp in (h ^ 1, 3 - h):
+                if not (hm >> (hp ^ 2)) & 1:
+                    out.append(("OFF", hp))
+        return out
+
+    def close(k, nd, used, cur):
+        for s in sorts(*cur[1:]):
+            off, onm, ons = used
+            if s == "ONS":
+                ons += 1
+            elif s == "ONM":
+                onm += 1
+            else:
+                off += 1
+            if off > 4 or onm > 4 or ons > 3 or off + onm + ons > 8:
+                continue
+            rest = () if k == n else walk(k, nd, (off, onm, ons), None)
+            if rest is not None:
+                return (("close", s),) + rest
+        return None
+
+    def walk(k, nd, used, cur):
+        key = (k, nd, used, cur)
+        if key not in memo:
+            memo[key] = step(k, nd, used, cur)
+        return memo[key]
+
+    def step(k, nd, used, cur):
+        if k == n:
+            return () if cur is None else close(k, nd, used, cur)
+        if kind[k] == "D" and nd < max_direct:
+            rest = walk(k + 1, nd + 1, used, cur)
+            if rest is not None:
+                return (("direct", k),) + rest
+        own = kind[k] == "S"
+        if cur is not None and k - cur[0] < width:
+            new = (cur[0], cur[1] + (not own), cur[2] + own, cur[3] or kind[k] == "X", cur[4] or kind[k] == "O",
+                   cur[5] | (1 << host_of[k]))
+            if sorts(*new[1:]):
+                rest = walk(k + 1, nd, used, new)
+                if rest is not None:
+                    return (("add", k),) + rest
+        if cur is not None:
+            return close(k, nd, used, cur)
+        new = (k, int(not own), int(own), kind[k] == "X", kind[k] == "O", 1 << host_of[k])
+        rest = walk(k + 1, nd, used, new)
+        return None if rest is None else (("add", k),) + rest
+
+    return walk(0, 0, (0, 0, 0), None)
+
+
+def build_plan(cores, route, topo):
+    n = len(cores)
+    cols = [[] for e in range(n)]
+    for r in range(n):
+        for t in range(TOK):
+            for j, e in enumerate(route[r][t]):
+                cols[e].append((r, j * TOK + t))
+    jobs = {c: {"rank": i, "windows": [], "direct": [], "arrive": 0} for i, c in enumerate(cores)}
+
+    def sends(src, items, base):
+        out = []
+        for (k, r, slot), (m, s) in zip(items, masks(len(items), base)):
+            assert topo.may_write(src, cores[r]) and m & ~topo.mask(src, cores[r]) == 0
+            jobs[cores[r]]["arrive"] += s
+            out.append((k, cores[r], slot, m, s))
+        return out
+
+    for e, me in enumerate(cores):
+        h, chip0 = topo.host(me), me - me % 8
+        kind, host_of = [], []
+        for r, slot in cols[e]:
+            hr = topo.host(cores[r])
+            host_of.append(hr)
+            kind.append("S" if r == e else "X" if hr == h ^ 2 else "D" if topo.may_write(me, cores[r]) else "O")
+        steps = None
+        for max_direct in (0, 4, 6, 8):
+            for width in range(4, WMAX + 1):
+                steps = group_columns(kind, host_of, h, width, max_direct)
+                if steps is not None:
+                    break
+            if steps is not None:
+                break
+        assert steps is not None
+        free = {"ONM": [2, 6, 3, 7], "ONS": [0, 4, 5], h ^ 1: [6, 2, 7, 3], 3 - h: [6, 2, 7, 3]}
+        groups, cur, direct = [], [], []
+        for what, arg in steps:
+            if what == "direct":
+                direct.append(arg)
+            elif what == "add":
+                cur.append(arg)
+            else:
+                if arg in ("ONM", "ONS"):
+                    fw = chip0 + free[arg].pop(0)
+                else:
+                    hp = arg[1]
+                    fw = hp * 128 + (topo.chip(me) + (4 if hp == h ^ 1 else 8)) * 8 + free[hp].pop(0)
+                groups.append((fw, cur))
+                cur = []
+        away = [q for q in groups if q[0] // 8 != me // 8]
+        home = [q for q in groups if q[0] // 8 == me // 8]
+        best = min(range(len(home) + 1), key=lambda x: max(rows(len(away) + x), rows(len(home) - x)))
+        low, high = away + home[:best], home[best:]
+        for part, base in ((low, 0), (high, 8)):
+            for (fw, ks), (m, s) in zip(part, masks(len(part), base)):
+                start = min(ks[0], ZCOLS - width)
+                assert ks[-1] - start < width
+                assert topo.may_write(me, fw) and m & ~topo.mask(me, fw) == 0 and fw not in jobs
+                jobs[me]["windows"].append((start, width, fw, m, s))
+                far = [(k - start,) + cols[e][k] for k in ks if cores[cols[e][k][0]] // 8 != fw // 8]
+                near = [(k - start,) + cols[e][k] for k in ks if cores[cols[e][k][0]] // 8 == fw // 8]
+                jobs[fw] = {"rank": None, "wait": s, "sends": sends(fw, far, 0) + sends(fw, near, 8)}
+        jobs[me]["direct"] = sends(me, [(k,) + cols[e][k] for k in direct], 0)
+    return jobs
+
+
+def column_call(g, core, T, topo, src, items):
+    trs = []
+    for k, dst, slot, m, s in items:
+        rid, pid = topo.addr(dst, core)
+        trs.append(RemoteDMATransfer(dst_ids=[DstId(rid=rid, pnc=pid)], dma_engine_mask=m, remote_sem=T.sem.arr,
+                                     src=src[:, k:k + 1], dst=T.AB[:, slot:slot + 1]))
+    g.remote_dma_fused(trs, local_sem=T.sem.sent)
+    return sum(s for k, dst, slot, m, s in items)
+
+
+def rank_program(g, core, T, topo):
+    if not PLAN:
+        PLAN.update(build_plan(list(T.cores), T.tables["ROUTE"], topo))
+    job = PLAN.get(core)
+    if job is None:
+        return
+
+    if job["rank"] is None:
+        g.wait_ge(T.sem.got, job["wait"])
+        left = column_call(g, core, T, topo, T.win, job["sends"])
+        g.wait_ge(T.sem.sent, left)
+        return
+
+    g.dma_start(T.Z[:], T.z[:]).then_inc(T.sem.ld, 16)
+    g.wait_ge(T.sem.ld, 16)
+    trs, left = [], 0
+    for start, width, fw, m, s in job["windows"]:
+        rid, pid = topo.addr(fw, core)
+        trs.append(RemoteDMATransfer(dst_ids=[DstId(rid=rid, pnc=pid)], dma_engine_mask=m, remote_sem=T.sem.got,
+                                     src=T.Z[:, start:start + width], dst=T.win[:, 0:width]))
+        left += s
+    g.remote_dma_fused(trs, local_sem=T.sem.sent)
+    if job["direct"]:
+        left += column_call(g, core, T, topo, T.Z, job["direct"])
+
+    g.wait_ge(T.sem.arr, job["arrive"])
+    g.dma_start(T.AB[:, 0:TOK], T.AB[:, TOK:2 * TOK], accum_op=AluOpType.add).then_inc(T.sem.ld, 16)
+    g.wait_ge(T.sem.ld, 32)
+    g.dma_start(T.y[:], T.AB[:, 0:TOK]).then_inc(T.sem.ld, 16)
+    g.wait_ge(T.sem.ld, 48)
+    g.wait_ge(T.sem.sent, left)

@@ -10,7 +10,7 @@ SCRATCH = {
     "win": ("sbuf", [128, WMAX], "bfloat16"),
     "AB": ("sbuf", [128, 2 * TOK], "bfloat16"),
 }
-SEMAPHORES = ["ld", "sent", "got", "arr"]
+SEMAPHORES = ["ld", "sent", "got", "arr_a", "arr_b"]
 
 PLAN = {}
 
@@ -105,21 +105,22 @@ def build_plan(cores, route, topo):
     for r in range(n):
         for t in range(TOK):
             for j, e in enumerate(route[r][t]):
-                cols[e].append((r, j * TOK + t))
-    jobs = {c: {"rank": i, "windows": [], "direct": [], "arrive": 0} for i, c in enumerate(cores)}
+                cols[e].append((r, t, j))
+    jobs = {c: {"role": "rank", "windows": [], "direct": [], "arrive": [0, 0]} for c in cores}
+    calls = []
+    cost = {}
 
-    def sends(src, items, base):
+    def spread(e, items, base, before):
         out = []
-        for (k, r, slot), (m, s) in zip(items, masks(len(items), base)):
-            assert topo.may_write(src, cores[r]) and m & ~topo.mask(src, cores[r]) == 0
-            jobs[cores[r]]["arrive"] += s
-            out.append((k, cores[r], slot, m, s))
+        for (pos, k), (m, s) in zip(items, masks(len(items), base)):
+            cost[cols[e][k]] = before + 128 // s
+            out.append((pos, e, k, m, s))
         return out
 
     for e, me in enumerate(cores):
         h, chip0 = topo.host(me), me - me % 8
         kind, host_of = [], []
-        for r, slot in cols[e]:
+        for r, t, j in cols[e]:
             hr = topo.host(cores[r])
             host_of.append(hr)
             kind.append("S" if r == e else "X" if hr == h ^ 2 else "D" if topo.may_write(me, cores[r]) else "O")
@@ -157,21 +158,32 @@ def build_plan(cores, route, topo):
                 assert ks[-1] - start < width
                 assert topo.may_write(me, fw) and m & ~topo.mask(me, fw) == 0 and fw not in jobs
                 jobs[me]["windows"].append((start, width, fw, m, s))
-                far = [(k - start,) + cols[e][k] for k in ks if cores[cols[e][k][0]] // 8 != fw // 8]
-                near = [(k - start,) + cols[e][k] for k in ks if cores[cols[e][k][0]] // 8 == fw // 8]
-                jobs[fw] = {"rank": None, "wait": s, "sends": sends(fw, far, 0) + sends(fw, near, 8)}
-        jobs[me]["direct"] = sends(me, [(k,) + cols[e][k] for k in direct], 0)
+                far = [(k - start, k) for k in ks if cores[cols[e][k][0]] // 8 != fw // 8]
+                near = [(k - start, k) for k in ks if cores[cols[e][k][0]] // 8 == fw // 8]
+                jobs[fw] = {"role": "forwarder", "wait": s, "sends": []}
+                calls.append((fw, jobs[fw]["sends"], spread(e, far, 0, 128 // s) + spread(e, near, 8, 128 // s)))
+        calls.append((me, jobs[me]["direct"], spread(e, [(k, k) for k in direct], 0, rows(len(low)))))
+
+    for src, out, items in calls:
+        for pos, e, k, m, s in items:
+            r, t, j = cols[e][k]
+            half = int((cost[(r, t, j)], j) > (cost[(r, t, 1 - j)], 1 - j))
+            assert topo.may_write(src, cores[r]) and m & ~topo.mask(src, cores[r]) == 0
+            jobs[cores[r]]["arrive"][half] += s
+            out.append((pos, cores[r], half, t, m, s))
     return jobs
 
 
 def column_call(g, core, T, topo, src, items):
     trs = []
-    for k, dst, slot, m, s in items:
+    for k, dst, half, t, m, s in items:
         rid, pid = topo.addr(dst, core)
-        trs.append(RemoteDMATransfer(dst_ids=[DstId(rid=rid, pnc=pid)], dma_engine_mask=m, remote_sem=T.sem.arr,
+        slot = half * TOK + t
+        trs.append(RemoteDMATransfer(dst_ids=[DstId(rid=rid, pnc=pid)], dma_engine_mask=m,
+                                     remote_sem=T.sem.arr_b if half else T.sem.arr_a,
                                      src=src[:, k:k + 1], dst=T.AB[:, slot:slot + 1]))
     g.remote_dma_fused(trs, local_sem=T.sem.sent)
-    return sum(s for k, dst, slot, m, s in items)
+    return sum(item[5] for item in items)
 
 
 def rank_program(g, core, T, topo):
@@ -181,7 +193,7 @@ def rank_program(g, core, T, topo):
     if job is None:
         return
 
-    if job["rank"] is None:
+    if job["role"] == "forwarder":
         g.wait_ge(T.sem.got, job["wait"])
         left = column_call(g, core, T, topo, T.win, job["sends"])
         g.wait_ge(T.sem.sent, left)
@@ -199,9 +211,10 @@ def rank_program(g, core, T, topo):
     if job["direct"]:
         left += column_call(g, core, T, topo, T.Z, job["direct"])
 
-    g.wait_ge(T.sem.arr, job["arrive"])
-    g.dma_start(T.AB[:, 0:TOK], T.AB[:, TOK:2 * TOK], accum_op=AluOpType.add).then_inc(T.sem.ld, 16)
-    g.wait_ge(T.sem.ld, 32)
+    g.wait_ge(T.sem.arr_a, job["arrive"][0])
     g.dma_start(T.y[:], T.AB[:, 0:TOK]).then_inc(T.sem.ld, 16)
+    g.wait_ge(T.sem.ld, 32)
+    g.wait_ge(T.sem.arr_b, job["arrive"][1])
+    g.dma_start(T.y[:], T.AB[:, TOK:2 * TOK], accum_op=AluOpType.add).then_inc(T.sem.ld, 16)
     g.wait_ge(T.sem.ld, 48)
     g.wait_ge(T.sem.sent, left)

from concourse.bass import DstId, RemoteDMATransfer
from concourse.mybir import AluOpType

TOK = 16
ZCOLS = 41
WMAX = 8

SCRATCH = {
    "Z": ("sbuf", [128, ZCOLS], "bfloat16"),
    "win": ("sbuf", [128, WMAX], "bfloat16"),
    "AB": ("sbuf", [128, 2 * TOK], "bfloat16"),
}
SEMAPHORES = ["ld", "sent", "got", "arr_a", "arr_b"]

PLAN = {}


def split(n, cap=8):
    size = [1] * n
    while n:
        i = min(range(n), key=lambda q: size[q])
        if sum(size) + size[i] > cap:
            break
        size[i] *= 2
    return size


def rows(n):
    return 128 // min(split(n)) if n else 0


def masks(n, base):
    out, bit = [], base
    for s in split(n):
        out.append((((1 << s) - 1) << bit, s))
        bit += s
    return out


def group_columns(kind, host_of, h, width, max_direct):
    n = len(kind)
    memo = {}

    def sorts(ns, nself, diag, odd, hm):
        out = []
        if not diag and ns <= 4 and nself <= 4:
            if not odd:
                out.append("ONS")
            out.append("ONM")
        if ns + nself <= 4:
            for hp in (h ^ 1, 3 - h):
                if not (hm >> (hp ^ 2)) & 1:
                    out.append(("OFF", hp))
        return out

    def close(k, nd, used, cur):
        for s in sorts(*cur[1:]):
            off, onm, ons = used
            if s == "ONS":
                ons += 1
            elif s == "ONM":
                onm += 1
            else:
                off += 1
            if off > 4 or onm > 4 or ons > 3 or off + onm + ons > 8:
                continue
            rest = () if k == n else walk(k, nd, (off, onm, ons), None)
            if rest is not None:
                return (("close", s),) + rest
        return None

    def walk(k, nd, used, cur):
        key = (k, nd, used, cur)
        if key not in memo:
            memo[key] = step(k, nd, used, cur)
        return memo[key]

    def step(k, nd, used, cur):
        if k == n:
            return () if cur is None else close(k, nd, used, cur)
        if kind[k] == "D" and nd < max_direct:
            rest = walk(k + 1, nd + 1, used, cur)
            if rest is not None:
                return (("direct", k),) + rest
        own = kind[k] == "S"
        if cur is not None and k - cur[0] < width:
            new = (cur[0], cur[1] + (not own), cur[2] + own, cur[3] or kind[k] == "X", cur[4] or kind[k] == "O",
                   cur[5] | (1 << host_of[k]))
            if sorts(*new[1:]):
                rest = walk(k + 1, nd, used, new)
                if rest is not None:
                    return (("add", k),) + rest
        if cur is not None:
            return close(k, nd, used, cur)
        new = (k, int(not own), int(own), kind[k] == "X", kind[k] == "O", 1 << host_of[k])
        rest = walk(k + 1, nd, used, new)
        return None if rest is None else (("add", k),) + rest

    return walk(0, 0, (0, 0, 0), None)


def build_plan(cores, route, topo):
    n = len(cores)
    cols = [[] for e in range(n)]
    for r in range(n):
        for t in range(TOK):
            for j, e in enumerate(route[r][t]):
                cols[e].append((r, t, j))
    jobs = {c: {"role": "rank", "windows": [], "direct": [], "arrive": [0, 0]} for c in cores}
    calls = []
    cost = {}

    def spread(e, items, base, before):
        out = []
        for (pos, k), (m, s) in zip(items, masks(len(items), base)):
            cost[cols[e][k]] = before + 128 // s
            out.append((pos, e, k, m, s))
        return out

    for e, me in enumerate(cores):
        h, chip0 = topo.host(me), me - me % 8
        kind, host_of = [], []
        for r, t, j in cols[e]:
            hr = topo.host(cores[r])
            host_of.append(hr)
            kind.append("S" if r == e else "X" if hr == h ^ 2 else "D" if topo.may_write(me, cores[r]) else "O")
        steps = None
        for max_direct in (0, 4, 6, 8):
            for width in range(4, WMAX + 1):
                steps = group_columns(kind, host_of, h, width, max_direct)
                if steps is not None:
                    break
            if steps is not None:
                break
        assert steps is not None
        free = {"ONM": [2, 6, 3, 7], "ONS": [0, 4, 5], h ^ 1: [6, 2, 7, 3], 3 - h: [6, 2, 7, 3]}
        groups, cur, direct = [], [], []
        for what, arg in steps:
            if what == "direct":
                direct.append(arg)
            elif what == "add":
                cur.append(arg)
            else:
                if arg in ("ONM", "ONS"):
                    fw = chip0 + free[arg].pop(0)
                else:
                    hp = arg[1]
                    fw = hp * 128 + (topo.chip(me) + (4 if hp == h ^ 1 else 8)) * 8 + free[hp].pop(0)
                groups.append((fw, cur))
                cur = []
        away = [q for q in groups if q[0] // 8 != me // 8]
        home = [q for q in groups if q[0] // 8 == me // 8]
        best = min(range(len(home) + 1), key=lambda x: max(rows(len(away) + x), rows(len(home) - x)))
        low, high = away + home[:best], home[best:]
        for part, base in ((low, 0), (high, 8)):
            for (fw, ks), (m, s) in zip(part, masks(len(part), base)):
                start = min(ks[0], ZCOLS - width)
                assert ks[-1] - start < width
                assert topo.may_write(me, fw) and m & ~topo.mask(me, fw) == 0 and fw not in jobs
                jobs[me]["windows"].append((start, width, fw, m, s))
                far = [(k - start, k) for k in ks if cores[cols[e][k][0]] // 8 != fw // 8]
                near = [(k - start, k) for k in ks if cores[cols[e][k][0]] // 8 == fw // 8]
                jobs[fw] = {"role": "forwarder", "wait": s, "sends": []}
                calls.append((fw, jobs[fw]["sends"], spread(e, far, 0, 128 // s) + spread(e, near, 8, 128 // s)))
        calls.append((me, jobs[me]["direct"], spread(e, [(k, k) for k in direct], 0, rows(len(low)))))

    for src, out, items in calls:
        for pos, e, k, m, s in items:
            r, t, j = cols[e][k]
            half = int((cost[(r, t, j)], j) > (cost[(r, t, 1 - j)], 1 - j))
            assert topo.may_write(src, cores[r]) and m & ~topo.mask(src, cores[r]) == 0
            jobs[cores[r]]["arrive"][half] += s
            out.append((pos, cores[r], half, t, m, s))
    return jobs


def column_call(g, core, T, topo, src, items):
    trs = []
    for k, dst, half, t, m, s in items:
        rid, pid = topo.addr(dst, core)
        slot = half * TOK + t
        trs.append(RemoteDMATransfer(dst_ids=[DstId(rid=rid, pnc=pid)], dma_engine_mask=m,
                                     remote_sem=T.sem.arr_b if half else T.sem.arr_a,
                                     src=src[:, k:k + 1], dst=T.AB[:, slot:slot + 1]))
    g.remote_dma_fused(trs, local_sem=T.sem.sent)
    return sum(item[5] for item in items)


def rank_program(g, core, T, topo):
    if not PLAN:
        PLAN.update(build_plan(list(T.cores), T.tables["ROUTE"], topo))
    job = PLAN.get(core)
    if job is None:
        return

    if job["role"] == "forwarder":
        g.wait_ge(T.sem.got, job["wait"])
        left = column_call(g, core, T, topo, T.win, job["sends"])
        g.wait_ge(T.sem.sent, left)
        return

    g.dma_start(T.Z[:], T.z[:]).then_inc(T.sem.ld, 16)
    g.wait_ge(T.sem.ld, 16)
    trs, left = [], 0
    for start, width, fw, m, s in job["windows"]:
        rid, pid = topo.addr(fw, core)
        trs.append(RemoteDMATransfer(dst_ids=[DstId(rid=rid, pnc=pid)], dma_engine_mask=m, remote_sem=T.sem.got,
                                     src=T.Z[:, start:start + width], dst=T.win[:, 0:width]))
        left += s
    g.remote_dma_fused(trs, local_sem=T.sem.sent)
    if job["direct"]:
        left += column_call(g, core, T, topo, T.Z, job["direct"])

    g.wait_ge(T.sem.arr_a, job["arrive"][0])
    g.dma_start(T.y[:], T.AB[:, 0:TOK]).then_inc(T.sem.ld, 16)
    g.wait_ge(T.sem.ld, 32)
    g.wait_ge(T.sem.arr_b, job["arrive"][1])
    g.dma_start(T.y[:], T.AB[:, TOK:2 * TOK], accum_op=AluOpType.add).then_inc(T.sem.ld, 16)
    g.wait_ge(T.sem.ld, 48)
    g.wait_ge(T.sem.sent, left)
